import numpy as np
import ml_dtypes


def mxq(x, axis, fmt="e4m3"):
    dtype, down = {"e4m3": (ml_dtypes.float8_e4m3fn, 7), "e5m2": (ml_dtypes.float8_e5m2, 14)}[fmt]
    v = np.moveaxis(np.asarray(x, np.float32).astype(ml_dtypes.bfloat16).astype(np.float64), axis, -1)
    blocks = v.reshape(v.shape[:-1] + (-1, 32))
    amax = np.abs(blocks).max(-1, keepdims=True)
    byte = np.maximum(np.where(amax > 0, np.frexp(amax)[1] - 1 + 127, 0) - down, 1)
    scale = np.exp2(byte - 127.0)
    codes = (blocks / scale).astype(np.float32).astype(dtype).astype(np.float64)
    return np.moveaxis((codes * scale).reshape(v.shape), -1, axis)


WIDE = False


def mx_kscale(k):
    if not WIDE:
        return np.ones(k)
    levels = np.array([10, -10, 5, -5, 0])
    if k % 512:
        return np.exp2(np.random.permutation(np.resize(levels, k // 32))).repeat(32)
    a = np.empty((k // 512, 16))
    for p in range(k // 512):
        a[p, :8] = np.random.permutation(np.resize(levels, 8))
        for g in range(8):
            far = levels[np.abs(levels - a[p, g]) >= 10]
            a[p, g + 8] = far[np.random.randint(len(far))]
    return np.exp2(a.ravel()).repeat(32)


def f64(x):
    return np.asarray(x).astype(np.float64)


def striped(idx):
    return np.tile(np.asarray(idx).reshape(-1, 16).T, (8, 1)).astype(np.uint16)


def unstriped(offs):
    return offs[:16].T.reshape(-1).astype(np.int64)


E2M1 = np.array([0.0, 0.5, 1.0, 1.5, 2.0, 3.0, 4.0, 6.0, -0.0, -0.5, -1.0, -1.5, -2.0, -3.0, -4.0, -6.0])


def pack_weight(w, fmt):
    k, n = w.shape
    w = f64(np.asarray(w, np.float32).astype(ml_dtypes.bfloat16)).reshape(k // 32, 32, n)
    amax = np.abs(w).max(1)
    if fmt == "e4m3":
        byte = np.frexp(amax)[1] - 1 + 127 - 7
    else:
        mant, ex = np.frexp(amax / 6.0)
        byte = np.where(mant > 0.5, ex, ex - 1) + 127
    byte = np.clip(np.where(amax > 0, byte, 1), 1, 254)
    scaled = (w * np.exp2(127.0 - byte)[:, None, :]).reshape(k, n).astype(np.float32)
    by_word = np.ascontiguousarray(scaled.reshape(k // 512, 128, 4, n).transpose(0, 1, 3, 2))
    if fmt == "e4m3":
        words = by_word.astype(ml_dtypes.float8_e4m3fn).view(np.uint8)
    else:
        c = by_word.astype(ml_dtypes.float4_e2m1fn).view(np.uint8) & 0xF
        words = (c[..., 0::2] | (c[..., 1::2] << 4)).reshape(k // 512, 128, 2 * n)
    return np.ascontiguousarray(words), np.ascontiguousarray(byte.astype(np.uint8).reshape(k // 512, 16, n))


def unpack_weight(words, scales, fmt):
    g, _, n = scales.shape
    words = np.ascontiguousarray(words).reshape(g, 128, n, -1)
    if fmt == "e4m3":
        vals = words.view(ml_dtypes.float8_e4m3fn).astype(np.float64)
    else:
        nib = np.empty((g, 128, n, 4), np.uint8)
        nib[..., 0::2] = words & 0xF
        nib[..., 1::2] = words >> 4
        vals = E2M1[nib]
    vals = vals * np.repeat(np.exp2(scales.astype(np.float64) - 127.0), 8, axis=1)[..., None]
    return vals.transpose(0, 1, 3, 2).reshape(g * 512, n)


D, T, I, Q = 512, 4096, 1024, 128


def setup_inputs():
    n = np.random.standard_normal
    idx = np.random.permutation(T)[:I]
    fd = mx_kscale(D)
    vocp = pack_weight(n((D, T)) / fd[:, None], "e4m3")
    return {
        "ha": (n((D, Q)) * 1.0 / np.sqrt(D) * fd[:, None]).astype(np.float32),
        "hb": (n((D, Q)) * 1.0 / np.sqrt(D) * fd[:, None]).astype(np.float32),
        "hc": (n((D, Q)) * 1.0 / np.sqrt(D) * fd[:, None]).astype(np.float32),
        "voc_words": vocp[0],
        "voc_scales": vocp[1],
        "pia": (np.random.uniform(0.2, 0.4, (Q, 1))).astype(np.float32),
        "pib": (np.random.uniform(0.2, 0.4, (Q, 1))).astype(np.float32),
        "pic": (np.random.uniform(0.2, 0.4, (Q, 1))).astype(np.float32),
        "offs": striped(idx),
    }


def reference(ha, hb, hc, voc_words, voc_scales, pia, pib, pic, offs):
    idx = unstriped(offs)
    vocu = unpack_weight(voc_words, voc_scales, "e4m3")
    haq = mxq(f64(ha), 0, "e4m3")
    vocidxg = vocu[:, idx]
    a = haq.T @ vocidxg
    hbq = mxq(f64(hb), 0, "e4m3")
    b = hbq.T @ vocidxg
    hcq = mxq(f64(hc), 0, "e4m3")
    r = hcq.T @ vocidxg
    pa = np.exp(a - np.max(a, axis=1, keepdims=True))
    pb = np.exp(b - np.max(b, axis=1, keepdims=True))
    pc = np.exp(r - np.max(r, axis=1, keepdims=True))
    y = (f64(pia) * pa / np.sum(pa, axis=1, keepdims=True) + f64(pib) * pb / np.sum(pb, axis=1, keepdims=True) + f64(pic) * pc / np.sum(pc, axis=1, keepdims=True)) * 512.0
    return y

@@ -1,0 +1,147 @@
+from contextlib import ExitStack
+
+import concourse.mybir as mybir
+
+F32 = mybir.dt.float32
+BF16 = mybir.dt.bfloat16
+U32 = mybir.dt.uint32
+I32 = mybir.dt.int32
+U16 = mybir.dt.uint16
+U8 = mybir.dt.uint8
+FP8X4 = mybir.dt.float8_e4m3fn_x4
+ALU = mybir.AluOpType
+ACT = mybir.ActivationFunctionType
+AX = mybir.AxisListType
+
+P = 128
+D, T, I, Q = 512, 4096, 1024, 128
+HALF = 512
+FLOPS = 3 * 2 * D * I * Q
+STORE = 256
+
+
+def tile_attend_mixsoftmax_kernel(tc, ha, hb, hc, voc_words, voc_scales, pia, pib, pic, offs, out):
+    nc = tc.nc
+    with ExitStack() as ctx:
+        sb = ctx.enter_context(tc.tile_pool(name="sb", bufs=1))
+        ps = ctx.enter_context(tc.psum_pool(name="ps", bufs=1))
+
+        offsets = sb.tile([P, I // 16], U16, name="offsets")
+        nc.sync.dma_start(offsets[:], offs)
+
+        words = sb.tile([P, T], I32, name="words", align_bytes=64)
+        nc.sync.dma_start(words[:], voc_words[0].rearrange("p n t -> p (n t)").bitcast(I32))
+
+        scales = sb.tile([P, T], U8, name="scales", tag="scales", align_bytes=64)
+        nc.vector.memset(scales[:].bitcast(I32), 0)
+        nc.scalar.dma_start(scales[0:P:8, :].bitcast(I32), voc_scales[0].bitcast(I32))
+
+        raw = []
+        for s, h in enumerate((ha, hb, hc)):
+            r = sb.tile([P, 4, Q], F32, name=f"raw{s}")
+            nc.sync.dma_start(r[:], h.rearrange("(p t) q -> p t q", t=4))
+            raw.append(r)
+
+        warm = sb.tile([P, 1], F32, name="warm")
+        nc.vector.memset(warm[:], 0.0)
+        warm2 = sb.tile([P, 1], F32, name="warm2")
+        nc.scalar.activation(warm2[:], warm[:], ACT.Exp)
+
+        vplane = sb.tile([P, I], U8, name="vplane", align_bytes=64)
+        nc.vector.memset(vplane[:].bitcast(I32), 0)
+
+        gscales = sb.tile([P, I], U8, name="gscales", tag="gscales", align_bytes=64)
+        nc.vector.tensor_copy(gscales[:], scales[:].indirect(offsets[:]))
+        for quad in range(4):
+            nc.sync.dma_start(
+                vplane[32 * quad : 32 * quad + 4, :].bitcast(I32),
+                gscales[32 * quad : 32 * quad + 32 : 8, :].bitcast(I32),
+            )
+
+        shares = sb.tile([P, 3, 8], F32, name="shares", tag="gscales", align_bytes=64)
+        for s, pi in enumerate((pia, pib, pic)):
+            nc.sync.dma_start(shares[:, s, 0:1], pi)
+
+        gwords = []
+        for u in range(2):
+            g = sb.tile([P, HALF], U32, name=f"gwords{u}", tag=("scales" if u == 0 else "gwords1"), align_bytes=64)
+            nc.vector.tensor_copy(g[:], words[:].bitcast(U32).indirect(offsets[:, u * 32 : (u + 1) * 32]))
+            gwords.append(g)
+
+        codes, planes = [], []
+        for s in range(3):
+            hb16 = sb.tile([P, Q, 4], BF16, name=f"hb16_{s}", align_bytes=64)
+            nc.scalar.copy(
+                hb16[:].rearrange("p (c i) t -> p c t i", i=4),
+                raw[s][:].rearrange("p t (c i) -> p c t i", i=4),
+            )
+            c = sb.tile([P, Q], U32, name=f"codes{s}", align_bytes=64)
+            pl = sb.tile([P, Q], U8, name=f"plane{s}", align_bytes=64)
+            nc.vector.quantize_mx(out=c[:].bitcast(FP8X4), scales=pl[:], in_=hb16[:].rearrange("p q t -> p (q t)"))
+            codes.append(c)
+            planes.append(pl)
+
+        banks, negmax0, negmax, negscores = {}, {}, {}, {}
+        probs, coefs = {}, {}
+
+        def score(s, u):
+            bank = ps.tile([P, HALF], F32, name=f"scores{s}_{u}")
+            nc.tensor.matmul_mx(
+                out=bank[:],
+                lhsT=codes[s][:].bitcast(FP8X4),
+                lhsT_scale=planes[s][:],
+                rhs=gwords[u][:].bitcast(FP8X4),
+                rhs_scale=vplane[:, u * HALF : (u + 1) * HALF],
+                start=True,
+                stop=True,
+            )
+            banks[s, u] = bank
+
+        def first_half(s):
+            score(s, 0)
+            nm = sb.tile([P, 1], F32, name=f"negmax0_{s}")
+            nc.vector.tensor_reduce(nm[:], banks[s, 0][:], AX.X, ALU.max, negate=True)
+            negmax0[s] = nm
+
+        def second_half(s):
+            score(s, 1)
+            nm = sb.tile([P, 1], F32, name=f"negmax_{s}")
+            ns = sb.tile([P, HALF], F32, name=f"negscores_{s}")
+            nc.vector.tensor_scalar(ns[:], banks[s, 1][:], -1.0, negmax0[s][:], ALU.mult, ALU.min, accum_out=nm[:])
+            p = sb.tile([P, I], F32, name=f"prob{s}")
+            t0 = sb.tile([P, 1], F32, name=f"total0_{s}")
+            t1 = sb.tile([P, 1], F32, name=f"total1_{s}")
+            nc.scalar.activation(p[:, :HALF], banks[s, 0][:], ACT.Exp, bias=nm[:], scale=1.0, accum_out=t0[:])
+            nc.scalar.activation(p[:, HALF:], ns[:], ACT.Exp, bias=nm[:], scale=-1.0, accum_out=t1[:])
+            probs[s] = (p, t0, t1)
+
+        def coefficient(s):
+            p, t0, t1 = probs[s]
+            total = sb.tile([P, 1], F32, name=f"total{s}")
+            nc.vector.tensor_tensor(total[:], t0[:], t1[:], ALU.add)
+            inv = sb.tile([P, 1], F32, name=f"inv{s}")
+            nc.vector.reciprocal(inv[:], total[:])
+            coef = sb.tile([P, 1], F32, name=f"coef{s}")
+            nc.vector.tensor_scalar(coef[:], inv[:], shares[:, s, 0:1], 512.0, ALU.mult, ALU.mult)
+            coefs[s] = coef
+
+        first_half(0)
+        first_half(1)
+        second_half(0)
+        first_half(2)
+        second_half(1)
+        second_half(2)
+
+        coefficient(0)
+        part_a = sb.tile([P, I], F32, name="part_a")
+        nc.vector.tensor_scalar(part_a[:], probs[0][0][:], coefs[0][:], None, ALU.mult)
+        coefficient(1)
+        part_ab = sb.tile([P, I], F32, name="part_ab")
+        nc.vector.scalar_tensor_tensor(part_ab[:], probs[1][0][:], coefs[1][:], part_a[:], ALU.mult, ALU.add)
+        coefficient(2)
+        for j in range(I // STORE):
+            cols = slice(j * STORE, (j + 1) * STORE)
+            res = sb.tile([P, STORE], F32, name=f"res{j}")
+            nc.vector.scalar_tensor_tensor(res[:], probs[2][0][:, cols], coefs[2][:], part_ab[:, cols], ALU.mult, ALU.add)
+            queue = nc.sync if j % 2 == 0 else nc.scalar
+            queue.dma_start(out[:, cols], res[:])

@@ -29,16 +29,16 @@ def tile_attend_mixsoftmax_kernel(tc, ha, hb, hc, voc_words, voc_scales, pia, pi
         offsets = sb.tile([P, I // 16], U16, name="offsets")
         nc.sync.dma_start(offsets[:], offs)
 
+        scales = sb.tile([P, T], U8, name="scales", tag="scales", align_bytes=64)
+        nc.sync.dma_start(scales[P - 16 : P, :].bitcast(I32), voc_scales[0].bitcast(I32))
+        nc.vector.memset(scales[0 : P - 16, :].bitcast(I32), 0)
+
         words = sb.tile([P, T], I32, name="words", align_bytes=64)
         nc.sync.dma_start(words[:], voc_words[0].rearrange("p n t -> p (n t)").bitcast(I32))
 
-        scales = sb.tile([P, T], U8, name="scales", tag="scales", align_bytes=64)
-        nc.vector.memset(scales[:].bitcast(I32), 0)
-        nc.scalar.dma_start(scales[0:P:8, :].bitcast(I32), voc_scales[0].bitcast(I32))
-
         raw = []
         for s, h in enumerate((ha, hb, hc)):
-            r = sb.tile([P, 4, Q], F32, name=f"raw{s}")
+            r = sb.tile([P, 4, Q], F32, name=f"raw{s}", tag=f"raw{s}", align_bytes=64)
             nc.sync.dma_start(r[:], h.rearrange("(p t) q -> p t q", t=4))
             raw.append(r)
 
@@ -53,23 +53,25 @@ def tile_attend_mixsoftmax_kernel(tc, ha, hb, hc, voc_words, voc_scales, pia, pi
         gscales = sb.tile([P, I], U8, name="gscales", tag="gscales", align_bytes=64)
         nc.vector.tensor_copy(gscales[:], scales[:].indirect(offsets[:]))
         for quad in range(4):
-            nc.sync.dma_start(
+            nc.scalar.dma_start(
                 vplane[32 * quad : 32 * quad + 4, :].bitcast(I32),
-                gscales[32 * quad : 32 * quad + 32 : 8, :].bitcast(I32),
+                gscales[P - 16 + 4 * quad : P - 12 + 4 * quad, :].bitcast(I32),
             )
 
         shares = sb.tile([P, 3, 8], F32, name="shares", tag="gscales", align_bytes=64)
         for s, pi in enumerate((pia, pib, pic)):
             nc.sync.dma_start(shares[:, s, 0:1], pi)
+        weights = sb.tile([P, 3], F32, name="weights")
+        nc.gpsimd.tensor_scalar(weights[:], shares[:, :, 0], 512.0, 0.0, ALU.mult, ALU.add)
 
-        gwords = []
-        for u in range(2):
-            g = sb.tile([P, HALF], U32, name=f"gwords{u}", tag=("scales" if u == 0 else "gwords1"), align_bytes=64)
+        gwords, codes, planes = {}, {}, {}
+
+        def gather_words(u, tag):
+            g = sb.tile([P, HALF], U32, name=f"gwords{u}", tag=tag, align_bytes=64)
             nc.vector.tensor_copy(g[:], words[:].bitcast(U32).indirect(offsets[:, u * 32 : (u + 1) * 32]))
-            gwords.append(g)
+            gwords[u] = g
 
-        codes, planes = [], []
-        for s in range(3):
+        def quantise(s):
             hb16 = sb.tile([P, Q, 4], BF16, name=f"hb16_{s}", align_bytes=64)
             nc.scalar.copy(
                 hb16[:].rearrange("p (c i) t -> p c t i", i=4),
@@ -78,8 +80,14 @@ def tile_attend_mixsoftmax_kernel(tc, ha, hb, hc, voc_words, voc_scales, pia, pi
             c = sb.tile([P, Q], U32, name=f"codes{s}", align_bytes=64)
             pl = sb.tile([P, Q], U8, name=f"plane{s}", align_bytes=64)
             nc.vector.quantize_mx(out=c[:].bitcast(FP8X4), scales=pl[:], in_=hb16[:].rearrange("p q t -> p (q t)"))
-            codes.append(c)
-            planes.append(pl)
+            codes[s] = c
+            planes[s] = pl
+
+        gather_words(0, "scales")
+        quantise(0)
+        gather_words(1, "raw0")
+        quantise(1)
+        quantise(2)
 
         banks, negmax0, negmax, negscores = {}, {}, {}, {}
         probs, coefs = {}, {}
@@ -97,51 +105,63 @@ def tile_attend_mixsoftmax_kernel(tc, ha, hb, hc, voc_words, voc_scales, pia, pi
             )
             banks[s, u] = bank
 
+        stats = {}
+
         def first_half(s):
+            nm = sb.tile([P, 2], F32, name=f"negmax_{s}")
+            tot = sb.tile([P, 2], F32, name=f"total_{s}")
+            p = sb.tile([P, I], F32, name=f"prob{s}")
             score(s, 0)
-            nm = sb.tile([P, 1], F32, name=f"negmax0_{s}")
-            nc.vector.tensor_reduce(nm[:], banks[s, 0][:], AX.X, ALU.max, negate=True)
-            negmax0[s] = nm
+            nc.vector.tensor_reduce(nm[:, 0:1], banks[s, 0][:], AX.X, ALU.max, negate=True)
+            nc.scalar.activation(p[:, :HALF], banks[s, 0][:], ACT.Exp, bias=nm[:, 0:1], scale=1.0, accum_out=tot[:, 0:1])
+            probs[s] = p
+            stats[s] = (nm, tot)
 
         def second_half(s):
+            nm, tot = stats[s]
             score(s, 1)
-            nm = sb.tile([P, 1], F32, name=f"negmax_{s}")
             ns = sb.tile([P, HALF], F32, name=f"negscores_{s}")
-            nc.vector.tensor_scalar(ns[:], banks[s, 1][:], -1.0, negmax0[s][:], ALU.mult, ALU.min, accum_out=nm[:])
-            p = sb.tile([P, I], F32, name=f"prob{s}")
-            t0 = sb.tile([P, 1], F32, name=f"total0_{s}")
-            t1 = sb.tile([P, 1], F32, name=f"total1_{s}")
-            nc.scalar.activation(p[:, :HALF], banks[s, 0][:], ACT.Exp, bias=nm[:], scale=1.0, accum_out=t0[:])
-            nc.scalar.activation(p[:, HALF:], ns[:], ACT.Exp, bias=nm[:], scale=-1.0, accum_out=t1[:])
-            probs[s] = (p, t0, t1)
+            nc.vector.tensor_scalar(ns[:], banks[s, 1][:], -1.0, nm[:, 0:1], ALU.mult, ALU.min, accum_out=nm[:, 1:2])
+            e = sb.tile([P, 2], F32, name=f"rescale_{s}")
+            nc.scalar.activation(e[:], nm[:], ACT.Exp, bias=nm[:, 1:2], scale=-1.0)
+            nc.scalar.activation(probs[s][:, HALF:], ns[:], ACT.Exp, bias=nm[:, 1:2], scale=-1.0, accum_out=tot[:, 1:2])
+            stats[s] = (nm, tot, e)
 
         def coefficient(s):
-            p, t0, t1 = probs[s]
-            total = sb.tile([P, 1], F32, name=f"total{s}")
-            nc.vector.tensor_tensor(total[:], t0[:], t1[:], ALU.add)
+            nm, tot, e = stats[s]
+            total = sb.tile([P, 1], F32, name=f"rowsum{s}")
+            nc.vector.tensor_scalar(total[:], tot[:, 0:1], e[:, 0:1], tot[:, 1:2], ALU.mult, ALU.add)
             inv = sb.tile([P, 1], F32, name=f"inv{s}")
             nc.vector.reciprocal(inv[:], total[:])
-            coef = sb.tile([P, 1], F32, name=f"coef{s}")
-            nc.vector.tensor_scalar(coef[:], inv[:], shares[:, s, 0:1], 512.0, ALU.mult, ALU.mult)
-            coefs[s] = coef
+            coef = sb.tile([P, 2], F32, name=f"coef{s}")
+            nc.vector.tensor_scalar(coef[:], e[:], inv[:], weights[:, s : s + 1], ALU.mult, ALU.mult)
+            return coef
 
         first_half(0)
         first_half(1)
         second_half(0)
+        coef_a = coefficient(0)
         first_half(2)
         second_half(1)
+        coef_b = coefficient(1)
         second_half(2)
+        coef_c = coefficient(2)
 
-        coefficient(0)
+        pa, pb, pc = probs[0], probs[1], probs[2]
         part_a = sb.tile([P, I], F32, name="part_a")
-        nc.vector.tensor_scalar(part_a[:], probs[0][0][:], coefs[0][:], None, ALU.mult)
-        coefficient(1)
         part_ab = sb.tile([P, I], F32, name="part_ab")
-        nc.vector.scalar_tensor_tensor(part_ab[:], probs[1][0][:], coefs[1][:], part_a[:], ALU.mult, ALU.add)
-        coefficient(2)
         for j in range(I // STORE):
             cols = slice(j * STORE, (j + 1) * STORE)
+            u = j * STORE // HALF
+            nc.vector.tensor_scalar(part_a[:, cols], pa[:, cols], coef_a[:, u : u + 1], None, ALU.mult)
+        for j in range(I // STORE):
+            cols = slice(j * STORE, (j + 1) * STORE)
+            u = j * STORE // HALF
+            nc.vector.scalar_tensor_tensor(part_ab[:, cols], pb[:, cols], coef_b[:, u : u + 1], part_a[:, cols], ALU.mult, ALU.add)
+        for j in range(I // STORE):
+            cols = slice(j * STORE, (j + 1) * STORE)
+            u = j * STORE // HALF
             res = sb.tile([P, STORE], F32, name=f"res{j}")
-            nc.vector.scalar_tensor_tensor(res[:], probs[2][0][:, cols], coefs[2][:], part_ab[:, cols], ALU.mult, ALU.add)
+            nc.vector.scalar_tensor_tensor(res[:], pc[:, cols], coef_c[:, u : u + 1], part_ab[:, cols], ALU.mult, ALU.add)
             queue = nc.sync if j % 2 == 0 else nc.scalar
             queue.dma_start(out[:, cols], res[:])

@@ -18,6 +18,7 @@ D, T, I, Q = 512, 4096, 1024, 128
 HALF = 512
 FLOPS = 3 * 2 * D * I * Q
 STORE = 256
+STORES = ((0, 256), (256, 512), (512, 832), (832, 1024))
 
 
 def tile_attend_mixsoftmax_kernel(tc, ha, hb, hc, voc_words, voc_scales, pia, pib, pic, offs, out):
@@ -30,17 +31,16 @@ def tile_attend_mixsoftmax_kernel(tc, ha, hb, hc, voc_words, voc_scales, pia, pi
         nc.sync.dma_start(offsets[:], offs)
 
         scales = sb.tile([P, T], U8, name="scales", tag="scales", align_bytes=64)
-        nc.sync.dma_start(scales[P - 16 : P, :].bitcast(I32), voc_scales[0].bitcast(I32))
+        nc.scalar.dma_start(scales[P - 16 : P, :].bitcast(I32), voc_scales[0].bitcast(I32))
         nc.vector.memset(scales[0 : P - 16, :].bitcast(I32), 0)
 
         words = sb.tile([P, T], I32, name="words", align_bytes=64)
         nc.sync.dma_start(words[:], voc_words[0].rearrange("p n t -> p (n t)").bitcast(I32))
 
-        raw = []
-        for s, h in enumerate((ha, hb, hc)):
-            r = sb.tile([P, 4, Q], F32, name=f"raw{s}", tag=f"raw{s}", align_bytes=64)
-            nc.sync.dma_start(r[:], h.rearrange("(p t) q -> p t q", t=4))
-            raw.append(r)
+        raw = [sb.tile([P, 4, Q], F32, name="raw0", tag="raw0", align_bytes=64)]
+        nc.sync.dma_start(raw[0][:], ha.rearrange("(p t) q -> p t q", t=4))
+        raw.append(sb.tile([P, 4, Q], F32, name="raw1"))
+        nc.sync.dma_start(raw[1][:], hb.rearrange("(p t) q -> p t q", t=4))
 
         warm = sb.tile([P, 1], F32, name="warm")
         nc.vector.memset(warm[:], 0.0)
@@ -53,10 +53,13 @@ def tile_attend_mixsoftmax_kernel(tc, ha, hb, hc, voc_words, voc_scales, pia, pi
         gscales = sb.tile([P, I], U8, name="gscales", tag="gscales", align_bytes=64)
         nc.vector.tensor_copy(gscales[:], scales[:].indirect(offsets[:]))
         for quad in range(4):
-            nc.scalar.dma_start(
+            nc.sync.dma_start(
                 vplane[32 * quad : 32 * quad + 4, :].bitcast(I32),
                 gscales[P - 16 + 4 * quad : P - 12 + 4 * quad, :].bitcast(I32),
             )
+
+        raw.append(sb.tile([P, 4, Q], F32, name="raw2", tag="scales", align_bytes=64))
+        nc.sync.dma_start(raw[2][:], hc.rearrange("(p t) q -> p t q", t=4))
 
         shares = sb.tile([P, 3, 8], F32, name="shares", tag="gscales", align_bytes=64)
         for s, pi in enumerate((pia, pib, pic)):
@@ -83,7 +86,7 @@ def tile_attend_mixsoftmax_kernel(tc, ha, hb, hc, voc_words, voc_scales, pia, pi
             codes[s] = c
             planes[s] = pl
 
-        gather_words(0, "scales")
+        gather_words(0, "gwords0")
         quantise(0)
         gather_words(1, "raw0")
         quantise(1)
@@ -127,41 +130,58 @@ def tile_attend_mixsoftmax_kernel(tc, ha, hb, hc, voc_words, voc_scales, pia, pi
             nc.scalar.activation(probs[s][:, HALF:], ns[:], ACT.Exp, bias=nm[:, 1:2], scale=-1.0, accum_out=tot[:, 1:2])
             stats[s] = (nm, tot, e)
 
-        def coefficient(s):
+        def row_sum(s):
             nm, tot, e = stats[s]
             total = sb.tile([P, 1], F32, name=f"rowsum{s}")
             nc.vector.tensor_scalar(total[:], tot[:, 0:1], e[:, 0:1], tot[:, 1:2], ALU.mult, ALU.add)
+            return total
+
+        def inverse(s, total):
             inv = sb.tile([P, 1], F32, name=f"inv{s}")
             nc.vector.reciprocal(inv[:], total[:])
+            return inv
+
+        def coefficient(s, inv):
             coef = sb.tile([P, 2], F32, name=f"coef{s}")
-            nc.vector.tensor_scalar(coef[:], e[:], inv[:], weights[:, s : s + 1], ALU.mult, ALU.mult)
+            nc.vector.tensor_scalar(coef[:], stats[s][2][:], inv[:], weights[:, s : s + 1], ALU.mult, ALU.mult)
             return coef
+
+        part_a = sb.tile([P, I], F32, name="part_a")
+        part_ab = sb.tile([P, I], F32, name="part_ab")
+
+        def scale_a(u):
+            cols = slice(u * HALF, (u + 1) * HALF)
+            nc.vector.tensor_scalar(part_a[:, cols], probs[0][:, cols], inv_a[:], share_a[:, u : u + 1], ALU.mult, ALU.mult)
+
+        def add_b(j):
+            cols = slice(j * STORE, (j + 1) * STORE)
+            u = j * STORE // HALF
+            nc.vector.scalar_tensor_tensor(part_ab[:, cols], probs[1][:, cols], coef_b[:, u : u + 1], part_a[:, cols], ALU.mult, ALU.add)
 
         first_half(0)
         first_half(1)
         second_half(0)
-        coef_a = coefficient(0)
-        first_half(2)
+        share_a = sb.tile([P, 2], F32, name="share_a")
+        nc.gpsimd.tensor_scalar(share_a[:], stats[0][2][:], weights[:, 0:1], 0.0, ALU.mult, ALU.add)
         second_half(1)
-        coef_b = coefficient(1)
+        first_half(2)
+        total_a = row_sum(0)
         second_half(2)
-        coef_c = coefficient(2)
-
-        pa, pb, pc = probs[0], probs[1], probs[2]
-        part_a = sb.tile([P, I], F32, name="part_a")
-        part_ab = sb.tile([P, I], F32, name="part_ab")
+        inv_a = inverse(0, total_a)
+        total_b = row_sum(1)
+        inv_b = inverse(1, total_b)
+        coef_b = coefficient(1, inv_b)
+        total_c = row_sum(2)
+        inv_c = inverse(2, total_c)
+        coef_c = coefficient(2, inv_c)
+        for u in range(2):
+            scale_a(u)
         for j in range(I // STORE):
-            cols = slice(j * STORE, (j + 1) * STORE)
-            u = j * STORE // HALF
-            nc.vector.tensor_scalar(part_a[:, cols], pa[:, cols], coef_a[:, u : u + 1], None, ALU.mult)
-        for j in range(I // STORE):
-            cols = slice(j * STORE, (j + 1) * STORE)
-            u = j * STORE // HALF
-            nc.vector.scalar_tensor_tensor(part_ab[:, cols], pb[:, cols], coef_b[:, u : u + 1], part_a[:, cols], ALU.mult, ALU.add)
-        for j in range(I // STORE):
-            cols = slice(j * STORE, (j + 1) * STORE)
-            u = j * STORE // HALF
-            res = sb.tile([P, STORE], F32, name=f"res{j}")
-            nc.vector.scalar_tensor_tensor(res[:], pc[:, cols], coef_c[:, u : u + 1], part_ab[:, cols], ALU.mult, ALU.add)
+            add_b(j)
+        for j, (lo, hi) in enumerate(STORES):
+            cols = slice(lo, hi)
+            u = lo // HALF
+            res = sb.tile([P, hi - lo], F32, name=f"res{j}")
+            nc.vector.scalar_tensor_tensor(res[:], probs[2][:, cols], coef_c[:, u : u + 1], part_ab[:, cols], ALU.mult, ALU.add)
             queue = nc.sync if j % 2 == 0 else nc.scalar
             queue.dma_start(out[:, cols], res[:])

@@ -14,11 +14,18 @@ ACT = mybir.ActivationFunctionType
 AX = mybir.AxisListType
 
 P = 128
-D, T, I, Q = 512, 4096, 1024, 128
-HALF = 512
-FLOPS = 3 * 2 * D * I * Q
-STORE = 256
+PACK = 4
+FEATURES, VOCAB, LISTED, ROWS = 512, 4096, 1024, 128
+STATES = 3
+BLOCKS = FEATURES // 32
+QUADRANT = 32
+HALF = LISTED // 2
+LIST_COLUMNS = HALF // 16
+OUT_SCALE = 512.0
+SHARE_PITCH = 8
+ADD_WIDTH = 256
 STORES = ((0, 256), (256, 512), (512, 832), (832, 1024))
+FLOPS = STATES * 2 * FEATURES * LISTED * ROWS
 
 
 def tile_attend_mixsoftmax_kernel(tc, ha, hb, hc, voc_words, voc_scales, pia, pib, pic, offs, out):
@@ -27,73 +34,78 @@ def tile_attend_mixsoftmax_kernel(tc, ha, hb, hc, voc_words, voc_scales, pia, pi
         sb = ctx.enter_context(tc.tile_pool(name="sb", bufs=1))
         ps = ctx.enter_context(tc.psum_pool(name="ps", bufs=1))
 
-        offsets = sb.tile([P, I // 16], U16, name="offsets")
+        offsets = sb.tile([P, LISTED // 16], U16, name="offsets")
         nc.sync.dma_start(offsets[:], offs)
 
-        scales = sb.tile([P, T], U8, name="scales", tag="scales", align_bytes=64)
-        nc.scalar.dma_start(scales[P - 16 : P, :].bitcast(I32), voc_scales[0].bitcast(I32))
-        nc.vector.memset(scales[0 : P - 16, :].bitcast(I32), 0)
+        first_scale_row = P - BLOCKS
+        scale_table = sb.tile([P, VOCAB], U8, name="scale_table", tag="scale_table", align_bytes=64)
+        nc.scalar.dma_start(scale_table[first_scale_row:P, :].bitcast(I32), voc_scales[0].bitcast(I32))
+        nc.vector.memset(scale_table[0:first_scale_row, :].bitcast(I32), 0)
 
-        words = sb.tile([P, T], I32, name="words", align_bytes=64)
-        nc.sync.dma_start(words[:], voc_words[0].rearrange("p n t -> p (n t)").bitcast(I32))
+        word_table = sb.tile([P, VOCAB], I32, name="word_table", align_bytes=64)
+        nc.sync.dma_start(word_table[:], voc_words[0].rearrange("p n t -> p (n t)").bitcast(I32))
 
-        raw = [sb.tile([P, 4, Q], F32, name="raw0", tag="raw0", align_bytes=64)]
-        nc.sync.dma_start(raw[0][:], ha.rearrange("(p t) q -> p t q", t=4))
-        raw.append(sb.tile([P, 4, Q], F32, name="raw1"))
-        nc.sync.dma_start(raw[1][:], hb.rearrange("(p t) q -> p t q", t=4))
+        hidden = {}
 
-        warm = sb.tile([P, 1], F32, name="warm")
-        nc.vector.memset(warm[:], 0.0)
-        warm2 = sb.tile([P, 1], F32, name="warm2")
-        nc.scalar.activation(warm2[:], warm[:], ACT.Exp)
+        def load_hidden(s, h, tag):
+            hidden[s] = sb.tile([P, PACK, ROWS], F32, name=f"hidden{s}", tag=tag, align_bytes=64)
+            nc.sync.dma_start(hidden[s][:], h.rearrange("(p t) q -> p t q", t=PACK))
 
-        vplane = sb.tile([P, I], U8, name="vplane", align_bytes=64)
-        nc.vector.memset(vplane[:].bitcast(I32), 0)
+        load_hidden(0, ha, "hidden0")
+        load_hidden(1, hb, "hidden1")
 
-        gscales = sb.tile([P, I], U8, name="gscales", tag="gscales", align_bytes=64)
-        nc.vector.tensor_copy(gscales[:], scales[:].indirect(offsets[:]))
-        for quad in range(4):
-            nc.sync.dma_start(
-                vplane[32 * quad : 32 * quad + 4, :].bitcast(I32),
-                gscales[P - 16 + 4 * quad : P - 12 + 4 * quad, :].bitcast(I32),
+        zero = sb.tile([P, 1], F32, name="zero")
+        nc.vector.memset(zero[:], 0.0)
+        rescale = [sb.tile([P, 2], F32, name=f"rescale{s}") for s in range(STATES)]
+        for s in range(STATES):
+            nc.scalar.activation(rescale[s][:, 1:2], zero[:], ACT.Exp)
+
+        voc_plane = sb.tile([P, LISTED], U8, name="voc_plane", align_bytes=64)
+        nc.vector.memset(voc_plane[:].bitcast(I32), 0)
+        listed_scales = sb.tile([P, LISTED], U8, name="listed_scales", tag="listed_scales", align_bytes=64)
+        nc.vector.tensor_copy(listed_scales[:], scale_table[:].indirect(offsets[:]))
+        for quad in range(P // QUADRANT):
+            queue = nc.scalar if quad == 0 else nc.sync
+            source = first_scale_row + 4 * quad
+            queue.dma_start(
+                voc_plane[QUADRANT * quad : QUADRANT * quad + 4, :].bitcast(I32),
+                listed_scales[source : source + 4, :].bitcast(I32),
             )
 
-        raw.append(sb.tile([P, 4, Q], F32, name="raw2", tag="scales", align_bytes=64))
-        nc.sync.dma_start(raw[2][:], hc.rearrange("(p t) q -> p t q", t=4))
+        load_hidden(2, hc, "scale_table")
 
-        shares = sb.tile([P, 3, 8], F32, name="shares", tag="gscales", align_bytes=64)
+        shares = sb.tile([P, STATES, SHARE_PITCH], F32, name="shares", tag="listed_scales", align_bytes=64)
         for s, pi in enumerate((pia, pib, pic)):
             nc.sync.dma_start(shares[:, s, 0:1], pi)
-        weights = sb.tile([P, 3], F32, name="weights")
-        nc.gpsimd.tensor_scalar(weights[:], shares[:, :, 0], 512.0, 0.0, ALU.mult, ALU.add)
+        weights = sb.tile([P, STATES], F32, name="weights")
+        nc.gpsimd.tensor_scalar(weights[:], shares[:, :, 0], OUT_SCALE, 0.0, ALU.mult, ALU.add)
 
-        gwords, codes, planes = {}, {}, {}
+        listed_words, codes, planes = {}, {}, {}
 
         def gather_words(u, tag):
-            g = sb.tile([P, HALF], U32, name=f"gwords{u}", tag=tag, align_bytes=64)
-            nc.vector.tensor_copy(g[:], words[:].bitcast(U32).indirect(offsets[:, u * 32 : (u + 1) * 32]))
-            gwords[u] = g
+            listed_words[u] = sb.tile([P, HALF], U32, name=f"listed_words{u}", tag=tag, align_bytes=64)
+            half_list = offsets[:, u * LIST_COLUMNS : (u + 1) * LIST_COLUMNS]
+            nc.vector.tensor_copy(listed_words[u][:], word_table[:].bitcast(U32).indirect(half_list))
 
         def quantise(s):
-            hb16 = sb.tile([P, Q, 4], BF16, name=f"hb16_{s}", align_bytes=64)
+            rounded = sb.tile([P, ROWS, PACK], BF16, name=f"rounded{s}", align_bytes=64)
             nc.scalar.copy(
-                hb16[:].rearrange("p (c i) t -> p c t i", i=4),
-                raw[s][:].rearrange("p t (c i) -> p c t i", i=4),
+                rounded[:].rearrange("p (c i) t -> p c t i", i=4),
+                hidden[s][:].rearrange("p t (c i) -> p c t i", i=4),
             )
-            c = sb.tile([P, Q], U32, name=f"codes{s}", align_bytes=64)
-            pl = sb.tile([P, Q], U8, name=f"plane{s}", align_bytes=64)
-            nc.vector.quantize_mx(out=c[:].bitcast(FP8X4), scales=pl[:], in_=hb16[:].rearrange("p q t -> p (q t)"))
-            codes[s] = c
-            planes[s] = pl
+            codes[s] = sb.tile([P, ROWS], U32, name=f"codes{s}", align_bytes=64)
+            planes[s] = sb.tile([P, ROWS], U8, name=f"plane{s}", align_bytes=64)
+            nc.vector.quantize_mx(
+                out=codes[s][:].bitcast(FP8X4), scales=planes[s][:], in_=rounded[:].rearrange("p q t -> p (q t)")
+            )
 
-        gather_words(0, "gwords0")
+        gather_words(0, "listed_words0")
         quantise(0)
-        gather_words(1, "raw0")
+        gather_words(1, "hidden0")
         quantise(1)
         quantise(2)
 
-        banks, negmax0, negmax, negscores = {}, {}, {}, {}
-        probs, coefs = {}, {}
+        negmax, sums, probs = {}, {}, {}
 
         def score(s, u):
             bank = ps.tile([P, HALF], F32, name=f"scores{s}_{u}")
@@ -101,87 +113,81 @@ def tile_attend_mixsoftmax_kernel(tc, ha, hb, hc, voc_words, voc_scales, pia, pi
                 out=bank[:],
                 lhsT=codes[s][:].bitcast(FP8X4),
                 lhsT_scale=planes[s][:],
-                rhs=gwords[u][:].bitcast(FP8X4),
-                rhs_scale=vplane[:, u * HALF : (u + 1) * HALF],
+                rhs=listed_words[u][:].bitcast(FP8X4),
+                rhs_scale=voc_plane[:, u * HALF : (u + 1) * HALF],
                 start=True,
                 stop=True,
             )
-            banks[s, u] = bank
-
-        stats = {}
+            return bank
 
         def first_half(s):
-            nm = sb.tile([P, 2], F32, name=f"negmax_{s}")
-            tot = sb.tile([P, 2], F32, name=f"total_{s}")
-            p = sb.tile([P, I], F32, name=f"prob{s}")
-            score(s, 0)
-            nc.vector.tensor_reduce(nm[:, 0:1], banks[s, 0][:], AX.X, ALU.max, negate=True)
-            nc.scalar.activation(p[:, :HALF], banks[s, 0][:], ACT.Exp, bias=nm[:, 0:1], scale=1.0, accum_out=tot[:, 0:1])
-            probs[s] = p
-            stats[s] = (nm, tot)
+            negmax[s] = sb.tile([P, 2], F32, name=f"negmax{s}")
+            sums[s] = sb.tile([P, 2], F32, name=f"sums{s}")
+            probs[s] = sb.tile([P, LISTED], F32, name=f"probs{s}")
+            bank = score(s, 0)
+            nc.vector.tensor_reduce(negmax[s][:, 0:1], bank[:], AX.X, ALU.max, negate=True)
+            nc.scalar.activation(
+                probs[s][:, :HALF], bank[:], ACT.Exp, bias=negmax[s][:, 0:1], scale=1.0, accum_out=sums[s][:, 0:1]
+            )
 
         def second_half(s):
-            nm, tot = stats[s]
-            score(s, 1)
-            ns = sb.tile([P, HALF], F32, name=f"negscores_{s}")
-            nc.vector.tensor_scalar(ns[:], banks[s, 1][:], -1.0, nm[:, 0:1], ALU.mult, ALU.min, accum_out=nm[:, 1:2])
-            e = sb.tile([P, 2], F32, name=f"rescale_{s}")
-            nc.scalar.activation(e[:], nm[:], ACT.Exp, bias=nm[:, 1:2], scale=-1.0)
-            nc.scalar.activation(probs[s][:, HALF:], ns[:], ACT.Exp, bias=nm[:, 1:2], scale=-1.0, accum_out=tot[:, 1:2])
-            stats[s] = (nm, tot, e)
+            bank = score(s, 1)
+            negated = sb.tile([P, HALF], F32, name=f"negated{s}")
+            nc.vector.tensor_scalar(
+                negated[:], bank[:], -1.0, negmax[s][:, 0:1], ALU.mult, ALU.min, accum_out=negmax[s][:, 1:2]
+            )
+            nc.scalar.activation(rescale[s][:, 0:1], negmax[s][:, 0:1], ACT.Exp, bias=negmax[s][:, 1:2], scale=-1.0)
+            nc.scalar.activation(
+                probs[s][:, HALF:], negated[:], ACT.Exp, bias=negmax[s][:, 1:2], scale=-1.0, accum_out=sums[s][:, 1:2]
+            )
 
         def row_sum(s):
-            nm, tot, e = stats[s]
-            total = sb.tile([P, 1], F32, name=f"rowsum{s}")
-            nc.vector.tensor_scalar(total[:], tot[:, 0:1], e[:, 0:1], tot[:, 1:2], ALU.mult, ALU.add)
+            total = sb.tile([P, 1], F32, name=f"total{s}")
+            nc.vector.tensor_scalar(total[:], sums[s][:, 0:1], rescale[s][:, 0:1], sums[s][:, 1:2], ALU.mult, ALU.add)
             return total
 
         def inverse(s, total):
-            inv = sb.tile([P, 1], F32, name=f"inv{s}")
+            inv = sb.tile([P, 1], F32, name=f"inverse{s}")
             nc.vector.reciprocal(inv[:], total[:])
             return inv
 
-        def coefficient(s, inv):
+        def coefficient(s):
+            inv = inverse(s, row_sum(s))
             coef = sb.tile([P, 2], F32, name=f"coef{s}")
-            nc.vector.tensor_scalar(coef[:], stats[s][2][:], inv[:], weights[:, s : s + 1], ALU.mult, ALU.mult)
+            nc.vector.tensor_scalar(coef[:], rescale[s][:], inv[:], weights[:, s : s + 1], ALU.mult, ALU.mult)
             return coef
 
-        part_a = sb.tile([P, I], F32, name="part_a")
-        part_ab = sb.tile([P, I], F32, name="part_ab")
-
-        def scale_a(u):
-            cols = slice(u * HALF, (u + 1) * HALF)
-            nc.vector.tensor_scalar(part_a[:, cols], probs[0][:, cols], inv_a[:], share_a[:, u : u + 1], ALU.mult, ALU.mult)
-
-        def add_b(j):
-            cols = slice(j * STORE, (j + 1) * STORE)
-            u = j * STORE // HALF
-            nc.vector.scalar_tensor_tensor(part_ab[:, cols], probs[1][:, cols], coef_b[:, u : u + 1], part_a[:, cols], ALU.mult, ALU.add)
+        term_a = sb.tile([P, LISTED], F32, name="term_a")
+        terms_ab = sb.tile([P, LISTED], F32, name="terms_ab")
 
         first_half(0)
         first_half(1)
         second_half(0)
-        share_a = sb.tile([P, 2], F32, name="share_a")
-        nc.gpsimd.tensor_scalar(share_a[:], stats[0][2][:], weights[:, 0:1], 0.0, ALU.mult, ALU.add)
+        weight_a = sb.tile([P, 2], F32, name="weight_a")
+        nc.gpsimd.tensor_scalar(weight_a[:], rescale[0][:], weights[:, 0:1], 0.0, ALU.mult, ALU.add)
         second_half(1)
         first_half(2)
         total_a = row_sum(0)
         second_half(2)
-        inv_a = inverse(0, total_a)
-        total_b = row_sum(1)
-        inv_b = inverse(1, total_b)
-        coef_b = coefficient(1, inv_b)
-        total_c = row_sum(2)
-        inv_c = inverse(2, total_c)
-        coef_c = coefficient(2, inv_c)
+        inverse_a = inverse(0, total_a)
+        coef_b = coefficient(1)
+        coef_c = coefficient(2)
+
         for u in range(2):
-            scale_a(u)
-        for j in range(I // STORE):
-            add_b(j)
+            cols = slice(u * HALF, (u + 1) * HALF)
+            nc.vector.tensor_scalar(
+                term_a[:, cols], probs[0][:, cols], inverse_a[:], weight_a[:, u : u + 1], ALU.mult, ALU.mult
+            )
+        for lo in range(0, LISTED, ADD_WIDTH):
+            cols, u = slice(lo, lo + ADD_WIDTH), lo // HALF
+            nc.vector.scalar_tensor_tensor(
+                terms_ab[:, cols], probs[1][:, cols], coef_b[:, u : u + 1], term_a[:, cols], ALU.mult, ALU.add
+            )
         for j, (lo, hi) in enumerate(STORES):
-            cols = slice(lo, hi)
-            u = lo // HALF
-            res = sb.tile([P, hi - lo], F32, name=f"res{j}")
-            nc.vector.scalar_tensor_tensor(res[:], probs[2][:, cols], coef_c[:, u : u + 1], part_ab[:, cols], ALU.mult, ALU.add)
+            cols, u = slice(lo, hi), lo // HALF
+            result = sb.tile([P, hi - lo], F32, name=f"result{j}")
+            nc.vector.scalar_tensor_tensor(
+                result[:], probs[2][:, cols], coef_c[:, u : u + 1], terms_ab[:, cols], ALU.mult, ALU.add
+            )
             queue = nc.sync if j % 2 == 0 else nc.scalar
-            queue.dma_start(out[:, cols], res[:])
+            queue.dma_start(out[:, cols], result[:])

from contextlib import ExitStack

import concourse.mybir as mybir

F32 = mybir.dt.float32
BF16 = mybir.dt.bfloat16
U32 = mybir.dt.uint32
I32 = mybir.dt.int32
U16 = mybir.dt.uint16
U8 = mybir.dt.uint8
FP8X4 = mybir.dt.float8_e4m3fn_x4
ALU = mybir.AluOpType
ACT = mybir.ActivationFunctionType
AX = mybir.AxisListType

P = 128
PACK = 4
FEATURES, VOCAB, LISTED, ROWS = 512, 4096, 1024, 128
STATES = 3
BLOCKS = FEATURES // 32
QUADRANT = 32
HALF = LISTED // 2
LIST_COLUMNS = HALF // 16
OUT_SCALE = 512.0
SHARE_PITCH = 8
ADD_WIDTH = 256
STORES = ((0, 256), (256, 512), (512, 832), (832, 1024))
FLOPS = STATES * 2 * FEATURES * LISTED * ROWS


def tile_attend_mixsoftmax_kernel(tc, ha, hb, hc, voc_words, voc_scales, pia, pib, pic, offs, out):
    nc = tc.nc
    with ExitStack() as ctx:
        sb = ctx.enter_context(tc.tile_pool(name="sb", bufs=1))
        ps = ctx.enter_context(tc.psum_pool(name="ps", bufs=1))

        offsets = sb.tile([P, LISTED // 16], U16, name="offsets")
        nc.sync.dma_start(offsets[:], offs)

        first_scale_row = P - BLOCKS
        scale_table = sb.tile([P, VOCAB], U8, name="scale_table", tag="scale_table", align_bytes=64)
        nc.scalar.dma_start(scale_table[first_scale_row:P, :].bitcast(I32), voc_scales[0].bitcast(I32))
        nc.vector.memset(scale_table[0:first_scale_row, :].bitcast(I32), 0)

        word_table = sb.tile([P, VOCAB], I32, name="word_table", align_bytes=64)
        nc.sync.dma_start(word_table[:], voc_words[0].rearrange("p n t -> p (n t)").bitcast(I32))

        hidden = {}

        def load_hidden(s, h, tag):
            hidden[s] = sb.tile([P, PACK, ROWS], F32, name=f"hidden{s}", tag=tag, align_bytes=64)
            nc.sync.dma_start(hidden[s][:], h.rearrange("(p t) q -> p t q", t=PACK))

        load_hidden(0, ha, "hidden0")
        load_hidden(1, hb, "hidden1")

        zero = sb.tile([P, 1], F32, name="zero")
        nc.vector.memset(zero[:], 0.0)
        rescale = [sb.tile([P, 2], F32, name=f"rescale{s}") for s in range(STATES)]
        for s in range(STATES):
            nc.scalar.activation(rescale[s][:, 1:2], zero[:], ACT.Exp)

        voc_plane = sb.tile([P, LISTED], U8, name="voc_plane", align_bytes=64)
        nc.vector.memset(voc_plane[:].bitcast(I32), 0)
        listed_scales = sb.tile([P, LISTED], U8, name="listed_scales", tag="listed_scales", align_bytes=64)
        nc.vector.tensor_copy(listed_scales[:], scale_table[:].indirect(offsets[:]))
        for quad in range(P // QUADRANT):
            queue = nc.scalar if quad == 0 else nc.sync
            source = first_scale_row + 4 * quad
            queue.dma_start(
                voc_plane[QUADRANT * quad : QUADRANT * quad + 4, :].bitcast(I32),
                listed_scales[source : source + 4, :].bitcast(I32),
            )

        load_hidden(2, hc, "scale_table")

        shares = sb.tile([P, STATES, SHARE_PITCH], F32, name="shares", tag="listed_scales", align_bytes=64)
        for s, pi in enumerate((pia, pib, pic)):
            nc.sync.dma_start(shares[:, s, 0:1], pi)
        weights = sb.tile([P, STATES], F32, name="weights")
        nc.gpsimd.tensor_scalar(weights[:], shares[:, :, 0], OUT_SCALE, 0.0, ALU.mult, ALU.add)

        listed_words, codes, planes = {}, {}, {}

        def gather_words(u, tag):
            listed_words[u] = sb.tile([P, HALF], U32, name=f"listed_words{u}", tag=tag, align_bytes=64)
            half_list = offsets[:, u * LIST_COLUMNS : (u + 1) * LIST_COLUMNS]
            nc.vector.tensor_copy(listed_words[u][:], word_table[:].bitcast(U32).indirect(half_list))

        def quantise(s):
            rounded = sb.tile([P, ROWS, PACK], BF16, name=f"rounded{s}", align_bytes=64)
            nc.scalar.copy(
                rounded[:].rearrange("p (c i) t -> p c t i", i=4),
                hidden[s][:].rearrange("p t (c i) -> p c t i", i=4),
            )
            codes[s] = sb.tile([P, ROWS], U32, name=f"codes{s}", align_bytes=64)
            planes[s] = sb.tile([P, ROWS], U8, name=f"plane{s}", align_bytes=64)
            nc.vector.quantize_mx(
                out=codes[s][:].bitcast(FP8X4), scales=planes[s][:], in_=rounded[:].rearrange("p q t -> p (q t)")
            )

        gather_words(0, "listed_words0")
        quantise(0)
        gather_words(1, "hidden0")
        quantise(1)
        quantise(2)

        negmax, sums, probs = {}, {}, {}

        def score(s, u):
            bank = ps.tile([P, HALF], F32, name=f"scores{s}_{u}")
            nc.tensor.matmul_mx(
                out=bank[:],
                lhsT=codes[s][:].bitcast(FP8X4),
                lhsT_scale=planes[s][:],
                rhs=listed_words[u][:].bitcast(FP8X4),
                rhs_scale=voc_plane[:, u * HALF : (u + 1) * HALF],
                start=True,
                stop=True,
            )
            return bank

        def first_half(s):
            negmax[s] = sb.tile([P, 2], F32, name=f"negmax{s}")
            sums[s] = sb.tile([P, 2], F32, name=f"sums{s}")
            probs[s] = sb.tile([P, LISTED], F32, name=f"probs{s}")
            bank = score(s, 0)
            nc.vector.tensor_reduce(negmax[s][:, 0:1], bank[:], AX.X, ALU.max, negate=True)
            nc.scalar.activation(
                probs[s][:, :HALF], bank[:], ACT.Exp, bias=negmax[s][:, 0:1], scale=1.0, accum_out=sums[s][:, 0:1]
            )

        def second_half(s):
            bank = score(s, 1)
            negated = sb.tile([P, HALF], F32, name=f"negated{s}")
            nc.vector.tensor_scalar(
                negated[:], bank[:], -1.0, negmax[s][:, 0:1], ALU.mult, ALU.min, accum_out=negmax[s][:, 1:2]
            )
            nc.scalar.activation(rescale[s][:, 0:1], negmax[s][:, 0:1], ACT.Exp, bias=negmax[s][:, 1:2], scale=-1.0)
            nc.scalar.activation(
                probs[s][:, HALF:], negated[:], ACT.Exp, bias=negmax[s][:, 1:2], scale=-1.0, accum_out=sums[s][:, 1:2]
            )

        def row_sum(s):
            total = sb.tile([P, 1], F32, name=f"total{s}")
            nc.vector.tensor_scalar(total[:], sums[s][:, 0:1], rescale[s][:, 0:1], sums[s][:, 1:2], ALU.mult, ALU.add)
            return total

        def inverse(s, total):
            inv = sb.tile([P, 1], F32, name=f"inverse{s}")
            nc.vector.reciprocal(inv[:], total[:])
            return inv

        def coefficient(s):
            inv = inverse(s, row_sum(s))
            coef = sb.tile([P, 2], F32, name=f"coef{s}")
            nc.vector.tensor_scalar(coef[:], rescale[s][:], inv[:], weights[:, s : s + 1], ALU.mult, ALU.mult)
            return coef

        term_a = sb.tile([P, LISTED], F32, name="term_a")
        terms_ab = sb.tile([P, LISTED], F32, name="terms_ab")

        first_half(0)
        first_half(1)
        second_half(0)
        weight_a = sb.tile([P, 2], F32, name="weight_a")
        nc.gpsimd.tensor_scalar(weight_a[:], rescale[0][:], weights[:, 0:1], 0.0, ALU.mult, ALU.add)
        second_half(1)
        first_half(2)
        total_a = row_sum(0)
        second_half(2)
        inverse_a = inverse(0, total_a)
        coef_b = coefficient(1)
        coef_c = coefficient(2)

        for u in range(2):
            cols = slice(u * HALF, (u + 1) * HALF)
            nc.vector.tensor_scalar(
                term_a[:, cols], probs[0][:, cols], inverse_a[:], weight_a[:, u : u + 1], ALU.mult, ALU.mult
            )
        for lo in range(0, LISTED, ADD_WIDTH):
            cols, u = slice(lo, lo + ADD_WIDTH), lo // HALF
            nc.vector.scalar_tensor_tensor(
                terms_ab[:, cols], probs[1][:, cols], coef_b[:, u : u + 1], term_a[:, cols], ALU.mult, ALU.add
            )
        for j, (lo, hi) in enumerate(STORES):
            cols, u = slice(lo, hi), lo // HALF
            result = sb.tile([P, hi - lo], F32, name=f"result{j}")
            nc.vector.scalar_tensor_tensor(
                result[:], probs[2][:, cols], coef_c[:, u : u + 1], terms_ab[:, cols], ALU.mult, ALU.add
            )
            queue = nc.sync if j % 2 == 0 else nc.scalar
            queue.dma_start(out[:, cols], result[:])
